import numpy as np
import ml_dtypes


def mxq(x, axis, fmt="e4m3"):
    dtype, down = {"e4m3": (ml_dtypes.float8_e4m3fn, 7), "e5m2": (ml_dtypes.float8_e5m2, 14)}[fmt]
    v = np.moveaxis(np.asarray(x, np.float32).astype(ml_dtypes.bfloat16).astype(np.float64), axis, -1)
    blocks = v.reshape(v.shape[:-1] + (-1, 32))
    amax = np.abs(blocks).max(-1, keepdims=True)
    byte = np.maximum(np.where(amax > 0, np.frexp(amax)[1] - 1 + 127, 0) - down, 1)
    scale = np.exp2(byte - 127.0)
    codes = (blocks / scale).astype(np.float32).astype(dtype).astype(np.float64)
    return np.moveaxis((codes * scale).reshape(v.shape), -1, axis)


WIDE = False


def mx_kscale(k):
    if not WIDE:
        return np.ones(k)
    levels = np.array([10, -10, 5, -5, 0])
    if k % 512:
        return np.exp2(np.random.permutation(np.resize(levels, k // 32))).repeat(32)
    a = np.empty((k // 512, 16))
    for p in range(k // 512):
        a[p, :8] = np.random.permutation(np.resize(levels, 8))
        for g in range(8):
            far = levels[np.abs(levels - a[p, g]) >= 10]
            a[p, g + 8] = far[np.random.randint(len(far))]
    return np.exp2(a.ravel()).repeat(32)


def f64(x):
    return np.asarray(x).astype(np.float64)


def striped(idx):
    return np.tile(idx.reshape(-1, 16).T, (8, 1)).astype(np.uint16)


def unstriped(offs):
    return offs[:16].T.reshape(-1).astype(np.int64)


def sigmoid(v):
    return 1.0 / (1.0 + np.exp(-np.maximum(v, -700.0)))


K, T, E, C, H, N = 1024, 640, 4, 128, 512, 512


def by_expert(wq, xq):
    return np.concatenate([wq[e].T @ xq[:, e * C:(e + 1) * C] for e in range(E)], axis=1)


def setup_inputs():
    n = np.random.standard_normal
    s = mx_kscale(K)[:, None]
    u = mx_kscale(H)
    return {
        "xT": (n((K, T)) * s).astype(np.float32),
        "w1": (n((E, K, H)) / np.sqrt(K) / s[None]).astype(np.float32),
        "w3": (n((E, K, H)) / np.sqrt(K) / s[None] * u[None, None, :]).astype(np.float32),
        "w2": (n((E, H, N)) / np.sqrt(H) / u[None, :, None]).astype(np.float32),
        "gate": np.tile(np.random.uniform(0.2, 1.0, E * C), (K, 1)).astype(np.float32),
        "offs": striped(np.random.permutation(T)[:E * C]),
    }


def reference(xT, w1, w3, w2, gate, offs):
    idx = unstriped(offs)
    xq = mxq(f64(gate) * f64(xT)[:, idx], 0, "e4m3")
    h = sigmoid(by_expert(mxq(f64(w1), 1, "e4m3"), xq))
    h = h * by_expert(mxq(f64(w3), 1, "e4m3"), xq)
    y = by_expert(mxq(f64(w2), 1, "e4m3"), mxq(h, 0, "e4m3"))
    out = np.zeros((N, T))
    out[:, idx] = y
    return out

@@ -1,0 +1,234 @@
+from contextlib import ExitStack
+
+import concourse.mybir as mybir
+
+K, T, E, C, H, N = 1024, 640, 4, 128, 512, 512
+S = E * C
+
+FLOPS = 2 * S * (2 * K * H + H * N)
+BYTES = 4 * (K * T + 2 * E * K * H + E * H * N + S + N * T) + 2 * 128 * (S // 16)
+
+F32 = mybir.dt.float32
+BF16 = mybir.dt.bfloat16
+U32 = mybir.dt.uint32
+U16 = mybir.dt.uint16
+U8 = mybir.dt.uint8
+FP8X4 = mybir.dt.float8_e4m3fn_x4
+MULT = mybir.AluOpType.mult
+SIGMOID = mybir.ActivationFunctionType.Sigmoid
+
+P = 128
+PACK = 4
+K_PASS = P * PACK
+PASSES = K // K_PASS
+WIDTH = 512
+HALF = WIDTH // 2
+OFFS_PER_EXPERT = C // 16
+ENG = [[("scalar", "scalar"), ("scalar", "scalar"), ("vector", "vector"), ("vector", "vector"), ("scalar", "scalar")],
+       [("scalar", "scalar"), ("vector", "vector"), ("scalar", "scalar"), ("vector", "vector"), ("scalar", "scalar")],
+       [("scalar", "scalar"), ("vector", "vector"), ("scalar", "scalar"), ("vector", "vector"), ("scalar", "scalar")],
+       [("scalar", "scalar"), ("vector", "vector"), ("scalar", "scalar"), ("scalar", "vector"), ("scalar", "scalar")]]
+
+PL = [0,2,6,8,8]
+XQ = [1,2]
+SG = [3,3,3,2]
+MU = [4,4,4,4]
+EV = [6,6,6]
+
+
+def tile_moe_pre_glu_sigmoid_kernel(tc, xT, w1, w3, w2, gate, offs, out):
+    nc = tc.nc
+
+    def copy_on(engine, dst, src):
+        if engine == "vector":
+            nc.vector.tensor_copy(out=dst, in_=src)
+        else:
+            nc.scalar.copy(out=dst, in_=src)
+
+    with ExitStack() as ctx:
+        keep = ctx.enter_context(tc.tile_pool(name="keep", bufs=1))
+        raws = ctx.enter_context(tc.tile_pool(name="raws", bufs=12))
+        stage = ctx.enter_context(tc.tile_pool(name="stage", bufs=4))
+        coded = ctx.enter_context(tc.tile_pool(name="coded", bufs=10))
+        small = ctx.enter_context(tc.tile_pool(name="small", bufs=2))
+        psum = ctx.enter_context(tc.psum_pool(name="psum", bufs=2))
+
+        offsets = keep.tile([P, S // 16], U16, name="offsets")
+        nc.sync.dma_start(offsets[:], offs)
+        gate_sb = keep.tile([P, S], F32, name="gate_sb")
+        nc.sync.dma_start(out=gate_sb[:], in_=gate[0:P, :])
+
+        warm = keep.tile([P, 1], F32, name="warm")
+        nc.vector.memset(warm[:], 0.0)
+        nc.scalar.activation(out=warm[:], in_=warm[:], func=SIGMOID)
+
+        out_tiles = [keep.tile([P, T], F32, name="out%d" % q) for q in range(N // P)]
+        for window in out_tiles:
+            nc.gpsimd.memset(window[:], 0.0)
+
+        x_rows = xT.rearrange("(g p j) t -> g j p t", p=P, j=PACK)
+        gathered = [keep.tile([P, PACK, S], F32, name="gathered%d" % g) for g in range(PASSES)]
+        x_codes = [keep.tile([P, S], U32, name="x_codes%d" % g, align_bytes=64) for g in range(PASSES)]
+        x_scales = [keep.tile([P, S], U8, name="x_scales%d" % g, align_bytes=64) for g in range(PASSES)]
+
+        def gather_plane(g, j):
+            plane = keep.tile([P, T], F32, name="x_plane%d_%d" % (g, j))
+            nc.sync.dma_start(out=plane[:], in_=x_rows[g, j])
+            nc.vector.tensor_tensor(gathered[g][:, j, :], plane[:].indirect(offsets[:]), gate_sb[:], MULT)
+
+        def quantize(grouped, codes, scales):
+            nc.vector.quantize_mx(out=codes.bitcast(FP8X4), scales=scales, in_=grouped)
+
+        def quantize_tokens(g):
+            grouped = stage.tile([P, PACK * S], BF16, name="grouped", align_bytes=64)
+            nc.scalar.copy(
+                out=grouped[:].rearrange("p (c i j) -> p c j i", i=4, j=PACK),
+                in_=gathered[g][:].rearrange("p j (c i) -> p c j i", i=4),
+            )
+            quantize(grouped[:], x_codes[g][:], x_scales[g][:])
+
+        def load(rows):
+            raw = raws.tile([P, PACK, WIDTH], F32, name="raw", align_bytes=64)
+            nc.sync.dma_start(out=raw[:], in_=rows.rearrange("(p j) w -> p j w", j=PACK))
+            return raw
+
+        def quantize_weights(raw, permute, engines, split):
+            grouped = stage.tile([P, PACK * WIDTH], BF16, name="grouped", align_bytes=64)
+            codes = coded.tile([P, WIDTH], U32, name="codes", align_bytes=64)
+            scales = coded.tile([P, WIDTH], U8, name="scales", align_bytes=64)
+            if engines[0] == engines[1] and permute:
+                copy_on(
+                    engines[0],
+                    grouped[:].rearrange("p (u t m j) -> p u m j t", u=2, t=2, j=PACK),
+                    raw[:].rearrange("p j (m u t) -> p u m j t", u=2, t=2),
+                )
+                engines = ()
+            elif engines[0] == engines[1]:
+                copy_on(
+                    engines[0],
+                    grouped[:].rearrange("p (c i j) -> p c j i", i=4, j=PACK),
+                    raw[:].rearrange("p j (c i) -> p c j i", i=4),
+                )
+                engines = ()
+            for u, engine in enumerate(engines):
+                dst = grouped[:, u * PACK * HALF : (u + 1) * PACK * HALF]
+                if permute:
+                    copy_on(
+                        engine,
+                        dst.rearrange("p (t m j) -> p m j t", t=2, j=PACK),
+                        raw[:].rearrange("p j (m t) -> p m j t", t=PACK)[:, :, :, 2 * u : 2 * u + 2],
+                    )
+                else:
+                    copy_on(
+                        engine,
+                        dst.rearrange("p (c i j) -> p c j i", i=4, j=PACK),
+                        raw[:, :, u * HALF : (u + 1) * HALF].rearrange("p j (c i) -> p c j i", i=4),
+                    )
+                if split:
+                    quantize(dst, codes[:, u * HALF : (u + 1) * HALF], scales[:, u * HALF : (u + 1) * HALF])
+            if not split:
+                quantize(grouped[:], codes[:], scales[:])
+            return codes, scales
+
+        def first_product(e, weights, name):
+            bank = psum.tile([P, PACK, C], F32, name=name)
+            for t in range(PACK):
+                for g in range(PASSES):
+                    codes, scales = weights[g]
+                    nc.tensor.matmul_mx(
+                        out=bank[:, t, :],
+                        lhsT=codes[:, t * P : (t + 1) * P].bitcast(FP8X4),
+                        lhsT_scale=scales[:, t * P : (t + 1) * P],
+                        rhs=x_codes[g][:, e * C : (e + 1) * C].bitcast(FP8X4),
+                        rhs_scale=x_scales[g][:, e * C : (e + 1) * C],
+                        start=(g == 0),
+                        stop=(g == PASSES - 1),
+                    )
+            return bank
+
+        def rows_of(w, e, g):
+            return w[e, g * K_PASS : (g + 1) * K_PASS, :]
+
+        def second_product(e, codes2, scales2, quarters):
+            h_codes, h_scales = h_packed[e]
+            bank = psum.tile([P, len(quarters), C], F32, name="y_bank")
+            for place, q in enumerate(quarters):
+                nc.tensor.matmul_mx(
+                    out=bank[:, place, :],
+                    lhsT=codes2[:, q * P : (q + 1) * P].bitcast(FP8X4),
+                    lhsT_scale=scales2[:, q * P : (q + 1) * P],
+                    rhs=h_codes[:].bitcast(FP8X4),
+                    rhs_scale=h_scales[:],
+                    start=True,
+                    stop=True,
+                )
+            return bank
+
+        def sigmoid_step(e, room):
+            a_bank = first_product(e, [packed[5 * e], packed[5 * e + 1]], "a_bank")
+            sigs[e] = room[:, 0, :].rearrange("p (c t) -> p c t", t=PACK)
+            nc.scalar.activation(out=sigs[e], in_=a_bank[:].rearrange("p t c -> p c t"), func=SIGMOID)
+
+        def hidden_step(e, room):
+            b_bank = first_product(e, [packed[5 * e + 2], packed[5 * e + 3]], "b_bank")
+            hidden = room[:, 1, 0:HALF].bitcast(BF16)
+            nc.vector.tensor_tensor(
+                hidden.rearrange("p (c t) -> p c t", t=PACK), b_bank[:].rearrange("p t c -> p c t"), sigs[e], MULT
+            )
+            h_codes = small.tile([P, C], U32, name="h_codes", align_bytes=64)
+            h_scales = small.tile([P, C], U8, name="h_scales", align_bytes=64)
+            quantize(hidden, h_codes[:], h_scales[:])
+            h_packed[e] = (h_codes, h_scales)
+
+        def leave_step(e, q, bank, place, y_sb):
+            nc.scalar.copy(out=y_sb, in_=bank[:, place, :])
+            slots = offsets[:, e * OFFS_PER_EXPERT : (e + 1) * OFFS_PER_EXPERT]
+            nc.vector.tensor_copy(out_tiles[q][:].indirect(slots), y_sb)
+
+        packed, sigs, h_packed, y_banks = {}, {}, {}, {}
+        planes = [(g, j) for g in range(PASSES) for j in range(PACK)]
+        final = 5 * E - 2
+        spare = keep.tile([P, PACK, WIDTH], F32, name="spare", align_bytes=64)
+        for s in range(final + 1):
+            e, n = divmod(s, 5)
+            if e == 0 and n < 4:
+                for plane in planes[PL[n] : PL[n + 1]]:
+                    gather_plane(*plane)
+            raw = load(w2[e] if n == 4 else rows_of(w1 if n < 2 else w3, e, n % 2))
+            if e == 0 and n in XQ:
+                quantize_tokens(XQ.index(n))
+            packed[s] = quantize_weights(raw, n < 4, ENG[e][n], s == final)
+            for d in range(E):
+                if min(5 * d + SG[d], final) == s:
+                    sigmoid_step(d, raw)
+                if d < E - 1:
+                    if 5 * d + MU[d] == s:
+                        hidden_step(d, raw)
+                    for q in range(PACK):
+                        if min(5 * d + EV[d] + q, final) == s:
+                            if q == 0:
+                                y_banks[d] = second_product(d, *packed[5 * d + 4], range(PACK))
+                            leave_step(d, q, y_banks[d], q, raw[:, 2, q * C : (q + 1) * C])
+
+        halves = []
+        for u in range(2):
+            half = keep.tile([P, PACK, HALF], F32, name="w2_last%d" % u)
+            nc.sync.dma_start(
+                out=half[:], in_=w2[E - 1].rearrange("(p j) w -> p j w", j=PACK)[:, :, u * HALF : (u + 1) * HALF]
+            )
+            halves.append(half)
+        hidden_step(E - 1, spare)
+        for u, half in enumerate(halves):
+            grouped = stage.tile([P, PACK * HALF], BF16, name="grouped", align_bytes=64)
+            codes = coded.tile([P, HALF], U32, name="codes", align_bytes=64)
+            scales = coded.tile([P, HALF], U8, name="scales", align_bytes=64)
+            nc.scalar.copy(
+                out=grouped[:].rearrange("p (c i j) -> p c j i", i=4, j=PACK),
+                in_=half[:].rearrange("p j (c i) -> p c j i", i=4),
+            )
+            quantize(grouped[:], codes[:], scales[:])
+            bank = second_product(E - 1, codes, scales, range(2))
+            for place in range(2):
+                q = 2 * u + place
+                leave_step(E - 1, q, bank, place, spare[:, 2, q * C : (q + 1) * C])
+                nc.sync.dma_start(out=out[q * P : (q + 1) * P, :], in_=out_tiles[q][:])

@@ -24,16 +24,17 @@ PASSES = K // K_PASS
 WIDTH = 512
 HALF = WIDTH // 2
 OFFS_PER_EXPERT = C // 16
-ENG = [[("scalar", "scalar"), ("scalar", "scalar"), ("vector", "vector"), ("vector", "vector"), ("scalar", "scalar")],
-       [("scalar", "scalar"), ("vector", "vector"), ("scalar", "scalar"), ("vector", "vector"), ("scalar", "scalar")],
-       [("scalar", "scalar"), ("vector", "vector"), ("scalar", "scalar"), ("vector", "vector"), ("scalar", "scalar")],
-       [("scalar", "scalar"), ("vector", "vector"), ("scalar", "scalar"), ("scalar", "vector"), ("scalar", "scalar")]]
+ENG = [[("vector", "vector"), ("scalar", "scalar"), ("scalar", "scalar"), ("vector", "vector"), ("scalar", "scalar")],
+       [("vector", "vector"), ("scalar", "scalar"), ("scalar", "scalar"), ("vector", "vector"), ("scalar", "scalar")],
+       [("vector", "vector"), ("scalar", "scalar"), ("scalar", "scalar"), ("vector", "vector"), ("scalar", "scalar")],
+       [("vector", "vector"), ("scalar", "scalar"), ("scalar", "scalar"), ("scalar", "vector"), ("scalar", "scalar")]]
 
-PL = [0,2,6,8,8]
+PL = [0,3,6,8,8,8]
 XQ = [1,2]
-SG = [3,3,3,2]
+SG = [4,4,4,3]
 MU = [4,4,4,4]
-EV = [6,6,6]
+EV = [[7,7,9,9],[7,7,9,9],[7,7,9,9]]
+XE = ["scalar","scalar"]
 
 
 def tile_moe_pre_glu_sigmoid_kernel(tc, xT, w1, w3, w2, gate, offs, out):
@@ -48,7 +49,7 @@ def tile_moe_pre_glu_sigmoid_kernel(tc, xT, w1, w3, w2, gate, offs, out):
     with ExitStack() as ctx:
         keep = ctx.enter_context(tc.tile_pool(name="keep", bufs=1))
         raws = ctx.enter_context(tc.tile_pool(name="raws", bufs=12))
-        stage = ctx.enter_context(tc.tile_pool(name="stage", bufs=4))
+        stage = ctx.enter_context(tc.tile_pool(name="stage", bufs=5))
         coded = ctx.enter_context(tc.tile_pool(name="coded", bufs=10))
         small = ctx.enter_context(tc.tile_pool(name="small", bufs=2))
         psum = ctx.enter_context(tc.psum_pool(name="psum", bufs=2))
@@ -56,7 +57,6 @@ def tile_moe_pre_glu_sigmoid_kernel(tc, xT, w1, w3, w2, gate, offs, out):
         offsets = keep.tile([P, S // 16], U16, name="offsets")
         nc.sync.dma_start(offsets[:], offs)
         gate_sb = keep.tile([P, S], F32, name="gate_sb")
-        nc.sync.dma_start(out=gate_sb[:], in_=gate[0:P, :])
 
         warm = keep.tile([P, 1], F32, name="warm")
         nc.vector.memset(warm[:], 0.0)
@@ -73,6 +73,8 @@ def tile_moe_pre_glu_sigmoid_kernel(tc, xT, w1, w3, w2, gate, offs, out):
 
         def gather_plane(g, j):
             plane = keep.tile([P, T], F32, name="x_plane%d_%d" % (g, j))
+            if (g, j) == (0, 0):
+                nc.sync.dma_start(out=gate_sb[:], in_=gate[0:P, :])
             nc.sync.dma_start(out=plane[:], in_=x_rows[g, j])
             nc.vector.tensor_tensor(gathered[g][:, j, :], plane[:].indirect(offsets[:]), gate_sb[:], MULT)
 
@@ -81,9 +83,10 @@ def tile_moe_pre_glu_sigmoid_kernel(tc, xT, w1, w3, w2, gate, offs, out):
 
         def quantize_tokens(g):
             grouped = stage.tile([P, PACK * S], BF16, name="grouped", align_bytes=64)
-            nc.scalar.copy(
-                out=grouped[:].rearrange("p (c i j) -> p c j i", i=4, j=PACK),
-                in_=gathered[g][:].rearrange("p j (c i) -> p c j i", i=4),
+            copy_on(
+                XE[g],
+                grouped[:].rearrange("p (c i j) -> p c j i", i=4, j=PACK),
+                gathered[g][:].rearrange("p j (c i) -> p c j i", i=4),
             )
             quantize(grouped[:], x_codes[g][:], x_scales[g][:])
 
@@ -96,14 +99,14 @@ def tile_moe_pre_glu_sigmoid_kernel(tc, xT, w1, w3, w2, gate, offs, out):
             grouped = stage.tile([P, PACK * WIDTH], BF16, name="grouped", align_bytes=64)
             codes = coded.tile([P, WIDTH], U32, name="codes", align_bytes=64)
             scales = coded.tile([P, WIDTH], U8, name="scales", align_bytes=64)
-            if engines[0] == engines[1] and permute:
+            if engines[0] == engines[1] and permute and not split:
                 copy_on(
                     engines[0],
                     grouped[:].rearrange("p (u t m j) -> p u m j t", u=2, t=2, j=PACK),
                     raw[:].rearrange("p j (m u t) -> p u m j t", u=2, t=2),
                 )
                 engines = ()
-            elif engines[0] == engines[1]:
+            elif engines[0] == engines[1] and not split:
                 copy_on(
                     engines[0],
                     grouped[:].rearrange("p (c i j) -> p c j i", i=4, j=PACK),
@@ -124,9 +127,11 @@ def tile_moe_pre_glu_sigmoid_kernel(tc, xT, w1, w3, w2, gate, offs, out):
                         dst.rearrange("p (c i j) -> p c j i", i=4, j=PACK),
                         raw[:, :, u * HALF : (u + 1) * HALF].rearrange("p j (c i) -> p c j i", i=4),
                     )
-                if split:
-                    quantize(dst, codes[:, u * HALF : (u + 1) * HALF], scales[:, u * HALF : (u + 1) * HALF])
-            if not split:
+            if split:
+                for u in range(2):
+                    cols = slice(u * HALF, (u + 1) * HALF)
+                    quantize(grouped[:, u * PACK * HALF : (u + 1) * PACK * HALF], codes[:, cols], scales[:, cols])
+            else:
                 quantize(grouped[:], codes[:], scales[:])
             return codes, scales
 
@@ -191,13 +196,13 @@ def tile_moe_pre_glu_sigmoid_kernel(tc, xT, w1, w3, w2, gate, offs, out):
         spare = keep.tile([P, PACK, WIDTH], F32, name="spare", align_bytes=64)
         for s in range(final + 1):
             e, n = divmod(s, 5)
-            if e == 0 and n < 4:
+            if e == 0:
                 for plane in planes[PL[n] : PL[n + 1]]:
                     gather_plane(*plane)
             raw = load(w2[e] if n == 4 else rows_of(w1 if n < 2 else w3, e, n % 2))
             if e == 0 and n in XQ:
                 quantize_tokens(XQ.index(n))
-            packed[s] = quantize_weights(raw, n < 4, ENG[e][n], s == final)
+            packed[s] = quantize_weights(raw, n < 4, ENG[e][n], "vector" in ENG[e][n])
             for d in range(E):
                 if min(5 * d + SG[d], final) == s:
                     sigmoid_step(d, raw)
@@ -205,7 +210,7 @@ def tile_moe_pre_glu_sigmoid_kernel(tc, xT, w1, w3, w2, gate, offs, out):
                     if 5 * d + MU[d] == s:
                         hidden_step(d, raw)
                     for q in range(PACK):
-                        if min(5 * d + EV[d] + q, final) == s:
+                        if min(5 * d + EV[d][q], final) == s:
                             if q == 0:
                                 y_banks[d] = second_product(d, *packed[5 * d + 4], range(PACK))
                             leave_step(d, q, y_banks[d], q, raw[:, 2, q * C : (q + 1) * C])

@@ -24,17 +24,16 @@ PASSES = K // K_PASS
 WIDTH = 512
 HALF = WIDTH // 2
 OFFS_PER_EXPERT = C // 16
-ENG = [[("vector", "vector"), ("scalar", "scalar"), ("scalar", "scalar"), ("vector", "vector"), ("scalar", "scalar")],
-       [("vector", "vector"), ("scalar", "scalar"), ("scalar", "scalar"), ("vector", "vector"), ("scalar", "scalar")],
-       [("vector", "vector"), ("scalar", "scalar"), ("scalar", "scalar"), ("vector", "vector"), ("scalar", "scalar")],
-       [("vector", "vector"), ("scalar", "scalar"), ("scalar", "scalar"), ("scalar", "vector"), ("scalar", "scalar")]]
-
+ENG = [[("scalar", "scalar"), ("scalar", "scalar"), ("scalar", "scalar"), ("vector", "vector"), ("vector", "scalar")],
+       [("scalar", "scalar"), ("vector", "scalar"), ("scalar", "scalar"), ("vector", "vector"), ("vector", "scalar")],
+       [("scalar", "scalar"), ("vector", "scalar"), ("scalar", "scalar"), ("vector", "vector"), ("vector", "scalar")],
+       [("scalar", "scalar"), ("vector", "scalar"), ("scalar", "scalar"), ("vector", "scalar"), ("scalar", "scalar")]]
 PL = [0,3,6,8,8,8]
 XQ = [1,2]
-SG = [4,4,4,3]
-MU = [4,4,4,4]
-EV = [[7,7,9,9],[7,7,9,9],[7,7,9,9]]
-XE = ["scalar","scalar"]
+SG = [2,2,2,2]
+MU = [3,3,3,4]
+EV = [[6,6,6,6],[6,6,6,6],[6,6,6,6]]
+XE = ["scalar","vector"]
 
 
 def tile_moe_pre_glu_sigmoid_kernel(tc, xT, w1, w3, w2, gate, offs, out):
@@ -85,8 +84,8 @@ def tile_moe_pre_glu_sigmoid_kernel(tc, xT, w1, w3, w2, gate, offs, out):
             grouped = stage.tile([P, PACK * S], BF16, name="grouped", align_bytes=64)
             copy_on(
                 XE[g],
-                grouped[:].rearrange("p (c i j) -> p c j i", i=4, j=PACK),
-                gathered[g][:].rearrange("p j (c i) -> p c j i", i=4),
+                grouped[:].rearrange("p (c i v w) -> p c v i w", i=4, v=2, w=2),
+                gathered[g][:].rearrange("p (v w) (c i) -> p c v i w", i=4, w=2),
             )
             quantize(grouped[:], x_codes[g][:], x_scales[g][:])
 
@@ -102,15 +101,15 @@ def tile_moe_pre_glu_sigmoid_kernel(tc, xT, w1, w3, w2, gate, offs, out):
             if engines[0] == engines[1] and permute and not split:
                 copy_on(
                     engines[0],
-                    grouped[:].rearrange("p (u t m j) -> p u m j t", u=2, t=2, j=PACK),
-                    raw[:].rearrange("p j (m u t) -> p u m j t", u=2, t=2),
+                    grouped[:].rearrange("p (t m v w) -> p m v t w", t=PACK, v=2, w=2),
+                    raw[:].rearrange("p (v w) (m t) -> p m v t w", t=PACK, w=2),
                 )
                 engines = ()
             elif engines[0] == engines[1] and not split:
                 copy_on(
                     engines[0],
-                    grouped[:].rearrange("p (c i j) -> p c j i", i=4, j=PACK),
-                    raw[:].rearrange("p j (c i) -> p c j i", i=4),
+                    grouped[:].rearrange("p (c i v w) -> p c v i w", i=4, v=2, w=2),
+                    raw[:].rearrange("p (v w) (c i) -> p c v i w", i=4, w=2),
                 )
                 engines = ()
             for u, engine in enumerate(engines):
@@ -118,14 +117,14 @@ def tile_moe_pre_glu_sigmoid_kernel(tc, xT, w1, w3, w2, gate, offs, out):
                 if permute:
                     copy_on(
                         engine,
-                        dst.rearrange("p (t m j) -> p m j t", t=2, j=PACK),
-                        raw[:].rearrange("p j (m t) -> p m j t", t=PACK)[:, :, :, 2 * u : 2 * u + 2],
+                        dst.rearrange("p (t m v w) -> p m v t w", t=2, v=2, w=2),
+                        raw[:].rearrange("p (v w) (m t) -> p m v t w", t=PACK, w=2)[:, :, :, 2 * u : 2 * u + 2, :],
                     )
                 else:
                     copy_on(
                         engine,
-                        dst.rearrange("p (c i j) -> p c j i", i=4, j=PACK),
-                        raw[:, :, u * HALF : (u + 1) * HALF].rearrange("p j (c i) -> p c j i", i=4),
+                        dst.rearrange("p (c i v w) -> p c v i w", i=4, v=2, w=2),
+                        raw[:, :, u * HALF : (u + 1) * HALF].rearrange("p (v w) (c i) -> p c v i w", i=4, w=2),
                     )
             if split:
                 for u in range(2):
@@ -176,7 +175,10 @@ def tile_moe_pre_glu_sigmoid_kernel(tc, xT, w1, w3, w2, gate, offs, out):
 
         def hidden_step(e, room):
             b_bank = first_product(e, [packed[5 * e + 2], packed[5 * e + 3]], "b_bank")
-            hidden = room[:, 1, 0:HALF].bitcast(BF16)
+            if room is None:
+                hidden = keep.tile([P, C * PACK], BF16, name="last_hidden", tag="handed_on", align_bytes=64)[:]
+            else:
+                hidden = room[:, 1, 0:HALF].bitcast(BF16)
             nc.vector.tensor_tensor(
                 hidden.rearrange("p (c t) -> p c t", t=PACK), b_bank[:].rearrange("p t c -> p c t"), sigs[e], MULT
             )
@@ -222,14 +224,18 @@ def tile_moe_pre_glu_sigmoid_kernel(tc, xT, w1, w3, w2, gate, offs, out):
                 out=half[:], in_=w2[E - 1].rearrange("(p j) w -> p j w", j=PACK)[:, :, u * HALF : (u + 1) * HALF]
             )
             halves.append(half)
-        hidden_step(E - 1, spare)
+        hidden_step(E - 1, None)
         for u, half in enumerate(halves):
             grouped = stage.tile([P, PACK * HALF], BF16, name="grouped", align_bytes=64)
-            codes = coded.tile([P, HALF], U32, name="codes", align_bytes=64)
+            if u == 0:
+                codes = coded.tile([P, HALF], U32, name="codes", align_bytes=64)
+            else:
+                codes = keep.tile([P, HALF], U32, name="last_codes", tag="handed_on", align_bytes=64)
             scales = coded.tile([P, HALF], U8, name="scales", align_bytes=64)
-            nc.scalar.copy(
-                out=grouped[:].rearrange("p (c i j) -> p c j i", i=4, j=PACK),
-                in_=half[:].rearrange("p j (c i) -> p c j i", i=4),
+            copy_on(
+                ENG[E - 1][4][u],
+                grouped[:].rearrange("p (c i v w) -> p c v i w", i=4, v=2, w=2),
+                half[:].rearrange("p (v w) (c i) -> p c v i w", i=4, w=2),
             )
             quantize(grouped[:], codes[:], scales[:])
             bank = second_product(E - 1, codes, scales, range(2))

@@ -1,6 +1,7 @@
 from contextlib import ExitStack
 
 import concourse.mybir as mybir
+from concourse.masks import make_identity
 
 K, T, E, C, H, N = 1024, 640, 4, 128, 512, 512
 S = E * C
@@ -23,35 +24,27 @@ K_PASS = P * PACK
 PASSES = K // K_PASS
 WIDTH = 512
 HALF = WIDTH // 2
-OFFS_PER_EXPERT = C // 16
-ENG = [[("scalar", "scalar"), ("scalar", "scalar"), ("scalar", "scalar"), ("vector", "vector"), ("vector", "scalar")],
-       [("scalar", "scalar"), ("vector", "scalar"), ("scalar", "scalar"), ("vector", "vector"), ("vector", "scalar")],
-       [("scalar", "scalar"), ("vector", "scalar"), ("scalar", "scalar"), ("vector", "vector"), ("vector", "scalar")],
-       [("scalar", "scalar"), ("vector", "scalar"), ("scalar", "scalar"), ("vector", "scalar"), ("scalar", "scalar")]]
-PL = [0,3,6,8,8,8]
-XQ = [1,2]
-SG = [2,2,2,2]
-MU = [3,3,3,4]
-EV = [[6,6,6,6],[6,6,6,6],[6,6,6,6]]
-XE = ["scalar","vector"]
+QUARTERS = N // P
+LIST_COLS = C // 16
+
+PLANES_AHEAD = 3
+
+RAW_BUFS, GROUPED_BUFS, PACKED_BUFS = 12, 5, 10
 
 
 def tile_moe_pre_glu_sigmoid_kernel(tc, xT, w1, w3, w2, gate, offs, out):
     nc = tc.nc
 
-    def copy_on(engine, dst, src):
-        if engine == "vector":
-            nc.vector.tensor_copy(out=dst, in_=src)
-        else:
-            nc.scalar.copy(out=dst, in_=src)
-
     with ExitStack() as ctx:
         keep = ctx.enter_context(tc.tile_pool(name="keep", bufs=1))
-        raws = ctx.enter_context(tc.tile_pool(name="raws", bufs=12))
-        stage = ctx.enter_context(tc.tile_pool(name="stage", bufs=5))
-        coded = ctx.enter_context(tc.tile_pool(name="coded", bufs=10))
+        raws = ctx.enter_context(tc.tile_pool(name="raws", bufs=RAW_BUFS))
+        stage = ctx.enter_context(tc.tile_pool(name="stage", bufs=GROUPED_BUFS))
+        coded = ctx.enter_context(tc.tile_pool(name="coded", bufs=PACKED_BUFS))
         small = ctx.enter_context(tc.tile_pool(name="small", bufs=2))
         psum = ctx.enter_context(tc.psum_pool(name="psum", bufs=2))
+
+        scalar_copy = nc.scalar.copy
+        vector_copy = nc.vector.tensor_copy
 
         offsets = keep.tile([P, S // 16], U16, name="offsets")
         nc.sync.dma_start(offsets[:], offs)
@@ -61,32 +54,48 @@ def tile_moe_pre_glu_sigmoid_kernel(tc, xT, w1, w3, w2, gate, offs, out):
         nc.vector.memset(warm[:], 0.0)
         nc.scalar.activation(out=warm[:], in_=warm[:], func=SIGMOID)
 
-        out_tiles = [keep.tile([P, T], F32, name="out%d" % q) for q in range(N // P)]
+        gate_cols = keep.tile([P, PACK], F32, name="gate_cols")
+        nc.sync.dma_start(out=gate_cols[:], in_=gate[0:1, :].rearrange("o (p r) -> (o p) r", r=PACK))
+        identity = keep.tile([P, P], F32, name="identity")
+        make_identity(nc, identity[:])
+        spread = psum.tile([P, PACK, P], F32, name="a_bank")
+        for r in range(PACK):
+            nc.tensor.transpose(spread[:, r, :], gate_cols[:, r : r + 1].to_broadcast([P, P]), identity[:])
+        vector_copy(out=gate_sb[:].rearrange("q (p r) -> q p r", r=PACK), in_=spread[:].rearrange("q r p -> q p r"))
+
+        out_tiles = [keep.tile([P, T], F32, name="out%d" % q) for q in range(QUARTERS)]
         for window in out_tiles:
             nc.gpsimd.memset(window[:], 0.0)
+
+        def quantize(grouped, codes, scales):
+            nc.vector.quantize_mx(out=codes.bitcast(FP8X4), scales=scales, in_=grouped)
+
+        def round_and_group(copy, grouped, rows):
+            copy(
+                out=grouped.rearrange("p (c i v w) -> p c v i w", i=4, v=2, w=2),
+                in_=rows.rearrange("p (v w) (c i) -> p c v i w", i=4, w=2),
+            )
+
+        def round_and_reorder(copy, grouped, raw, t0, t1):
+            copy(
+                out=grouped[:, t0 * PACK * P : t1 * PACK * P].rearrange("p (t m v w) -> p m v t w", m=P, v=2, w=2),
+                in_=raw.rearrange("p (v w) (m t) -> p m v t w", t=PACK, w=2)[:, :, :, t0:t1, :],
+            )
 
         x_rows = xT.rearrange("(g p j) t -> g j p t", p=P, j=PACK)
         gathered = [keep.tile([P, PACK, S], F32, name="gathered%d" % g) for g in range(PASSES)]
         x_codes = [keep.tile([P, S], U32, name="x_codes%d" % g, align_bytes=64) for g in range(PASSES)]
         x_scales = [keep.tile([P, S], U8, name="x_scales%d" % g, align_bytes=64) for g in range(PASSES)]
+        planes = [(g, j) for g in range(PASSES) for j in range(PACK)]
 
         def gather_plane(g, j):
-            plane = keep.tile([P, T], F32, name="x_plane%d_%d" % (g, j))
-            if (g, j) == (0, 0):
-                nc.sync.dma_start(out=gate_sb[:], in_=gate[0:P, :])
+            plane = keep.tile([P, T], F32, name="x_plane%d_%d" % (g, j), align_bytes=64)
             nc.sync.dma_start(out=plane[:], in_=x_rows[g, j])
             nc.vector.tensor_tensor(gathered[g][:, j, :], plane[:].indirect(offsets[:]), gate_sb[:], MULT)
 
-        def quantize(grouped, codes, scales):
-            nc.vector.quantize_mx(out=codes.bitcast(FP8X4), scales=scales, in_=grouped)
-
-        def quantize_tokens(g):
+        def quantize_tokens(g, copy):
             grouped = stage.tile([P, PACK * S], BF16, name="grouped", align_bytes=64)
-            copy_on(
-                XE[g],
-                grouped[:].rearrange("p (c i v w) -> p c v i w", i=4, v=2, w=2),
-                gathered[g][:].rearrange("p (v w) (c i) -> p c v i w", i=4, w=2),
-            )
+            round_and_group(copy, grouped[:], gathered[g][:])
             quantize(grouped[:], x_codes[g][:], x_scales[g][:])
 
         def load(rows):
@@ -94,152 +103,156 @@ def tile_moe_pre_glu_sigmoid_kernel(tc, xT, w1, w3, w2, gate, offs, out):
             nc.sync.dma_start(out=raw[:], in_=rows.rearrange("(p j) w -> p j w", j=PACK))
             return raw
 
-        def quantize_weights(raw, permute, engines, split):
-            grouped = stage.tile([P, PACK * WIDTH], BF16, name="grouped", align_bytes=64)
+        def packed_tiles():
             codes = coded.tile([P, WIDTH], U32, name="codes", align_bytes=64)
             scales = coded.tile([P, WIDTH], U8, name="scales", align_bytes=64)
-            if engines[0] == engines[1] and permute and not split:
-                copy_on(
-                    engines[0],
-                    grouped[:].rearrange("p (t m v w) -> p m v t w", t=PACK, v=2, w=2),
-                    raw[:].rearrange("p (v w) (m t) -> p m v t w", t=PACK, w=2),
-                )
-                engines = ()
-            elif engines[0] == engines[1] and not split:
-                copy_on(
-                    engines[0],
-                    grouped[:].rearrange("p (c i v w) -> p c v i w", i=4, v=2, w=2),
-                    raw[:].rearrange("p (v w) (c i) -> p c v i w", i=4, w=2),
-                )
-                engines = ()
-            for u, engine in enumerate(engines):
-                dst = grouped[:, u * PACK * HALF : (u + 1) * PACK * HALF]
-                if permute:
-                    copy_on(
-                        engine,
-                        dst.rearrange("p (t m v w) -> p m v t w", t=2, v=2, w=2),
-                        raw[:].rearrange("p (v w) (m t) -> p m v t w", t=PACK, w=2)[:, :, :, 2 * u : 2 * u + 2, :],
-                    )
+            return codes, scales
+
+        def pack_first_on_scalar(raw, codes, scales):
+            grouped = stage.tile([P, PACK * WIDTH], BF16, name="grouped", align_bytes=64)
+            round_and_reorder(scalar_copy, grouped[:], raw[:], 0, PACK)
+            quantize(grouped[:], codes[:], scales[:])
+            return codes, scales
+
+        def pack_in_halves(raw, copies, reorder):
+            grouped = stage.tile([P, PACK * WIDTH], BF16, name="grouped", align_bytes=64)
+            codes, scales = packed_tiles()
+            halves = [slice(u * HALF, (u + 1) * HALF) for u in range(2)]
+            grouped_halves = [grouped[:, u * PACK * HALF : (u + 1) * PACK * HALF] for u in range(2)]
+            for u, copy in enumerate(copies):
+                if reorder:
+                    round_and_reorder(copy, grouped[:], raw[:], 2 * u, 2 * u + 2)
                 else:
-                    copy_on(
-                        engine,
-                        dst.rearrange("p (c i v w) -> p c v i w", i=4, v=2, w=2),
-                        raw[:, :, u * HALF : (u + 1) * HALF].rearrange("p (v w) (c i) -> p c v i w", i=4, w=2),
-                    )
-            if split:
-                for u in range(2):
-                    cols = slice(u * HALF, (u + 1) * HALF)
-                    quantize(grouped[:, u * PACK * HALF : (u + 1) * PACK * HALF], codes[:, cols], scales[:, cols])
-            else:
-                quantize(grouped[:], codes[:], scales[:])
+                    round_and_group(copy, grouped_halves[u], raw[:, :, halves[u]])
+            for u in range(2):
+                quantize(grouped_halves[u], codes[:, halves[u]], scales[:, halves[u]])
             return codes, scales
 
         def first_product(e, weights, name):
             bank = psum.tile([P, PACK, C], F32, name=name)
+            slots = slice(e * C, (e + 1) * C)
             for t in range(PACK):
-                for g in range(PASSES):
-                    codes, scales = weights[g]
+                for g, (codes, scales) in enumerate(weights):
                     nc.tensor.matmul_mx(
                         out=bank[:, t, :],
                         lhsT=codes[:, t * P : (t + 1) * P].bitcast(FP8X4),
                         lhsT_scale=scales[:, t * P : (t + 1) * P],
-                        rhs=x_codes[g][:, e * C : (e + 1) * C].bitcast(FP8X4),
-                        rhs_scale=x_scales[g][:, e * C : (e + 1) * C],
+                        rhs=x_codes[g][:, slots].bitcast(FP8X4),
+                        rhs_scale=x_scales[g][:, slots],
                         start=(g == 0),
                         stop=(g == PASSES - 1),
                     )
             return bank
 
-        def rows_of(w, e, g):
-            return w[e, g * K_PASS : (g + 1) * K_PASS, :]
+        def sigmoid_of(e, weights, room):
+            a_bank = first_product(e, weights, "a_bank")
+            nc.scalar.activation(
+                out=room.rearrange("p (c t) -> p c t", t=PACK),
+                in_=a_bank[:].rearrange("p t c -> p c t"),
+                func=SIGMOID,
+            )
 
-        def second_product(e, codes2, scales2, quarters):
-            h_codes, h_scales = h_packed[e]
-            bank = psum.tile([P, len(quarters), C], F32, name="y_bank")
-            for place, q in enumerate(quarters):
+        def pack_hidden(e, weights, sig, hidden):
+            b_bank = first_product(e, weights, "b_bank")
+            nc.vector.tensor_tensor(
+                hidden.rearrange("p (c t) -> p c t", t=PACK),
+                b_bank[:].rearrange("p t c -> p c t"),
+                sig.rearrange("p (c t) -> p c t", t=PACK),
+                MULT,
+            )
+            h_codes = small.tile([P, C], U32, name="h_codes", align_bytes=64)
+            h_scales = small.tile([P, C], U8, name="h_scales", align_bytes=64)
+            quantize(hidden, h_codes[:], h_scales[:])
+            return h_codes, h_scales
+
+        def second_product(h_packed, weights, blocks):
+            codes, scales = weights
+            bank = psum.tile([P, blocks, C], F32, name="y_bank")
+            for b in range(blocks):
                 nc.tensor.matmul_mx(
-                    out=bank[:, place, :],
-                    lhsT=codes2[:, q * P : (q + 1) * P].bitcast(FP8X4),
-                    lhsT_scale=scales2[:, q * P : (q + 1) * P],
-                    rhs=h_codes[:].bitcast(FP8X4),
-                    rhs_scale=h_scales[:],
+                    out=bank[:, b, :],
+                    lhsT=codes[:, b * P : (b + 1) * P].bitcast(FP8X4),
+                    lhsT_scale=scales[:, b * P : (b + 1) * P],
+                    rhs=h_packed[0][:].bitcast(FP8X4),
+                    rhs_scale=h_packed[1][:],
                     start=True,
                     stop=True,
                 )
             return bank
 
-        def sigmoid_step(e, room):
-            a_bank = first_product(e, [packed[5 * e], packed[5 * e + 1]], "a_bank")
-            sigs[e] = room[:, 0, :].rearrange("p (c t) -> p c t", t=PACK)
-            nc.scalar.activation(out=sigs[e], in_=a_bank[:].rearrange("p t c -> p c t"), func=SIGMOID)
+        def scatter(e, q, y_psum, room):
+            scalar_copy(out=room, in_=y_psum)
+            vector_copy(out_tiles[q][:].indirect(offsets[:, e * LIST_COLS : (e + 1) * LIST_COLS]), room)
 
-        def hidden_step(e, room):
-            b_bank = first_product(e, [packed[5 * e + 2], packed[5 * e + 3]], "b_bank")
-            if room is None:
-                hidden = keep.tile([P, C * PACK], BF16, name="last_hidden", tag="handed_on", align_bytes=64)[:]
-            else:
-                hidden = room[:, 1, 0:HALF].bitcast(BF16)
-            nc.vector.tensor_tensor(
-                hidden.rearrange("p (c t) -> p c t", t=PACK), b_bank[:].rearrange("p t c -> p c t"), sigs[e], MULT
-            )
-            h_codes = small.tile([P, C], U32, name="h_codes", align_bytes=64)
-            h_scales = small.tile([P, C], U8, name="h_scales", align_bytes=64)
-            quantize(hidden, h_codes[:], h_scales[:])
-            h_packed[e] = (h_codes, h_scales)
+        shared = (vector_copy, scalar_copy)
+        h_packed = w2_packed = None
+        for e in range(E):
+            first = e == 0
+            last = e == E - 1
 
-        def leave_step(e, q, bank, place, y_sb):
-            nc.scalar.copy(out=y_sb, in_=bank[:, place, :])
-            slots = offsets[:, e * OFFS_PER_EXPERT : (e + 1) * OFFS_PER_EXPERT]
-            nc.vector.tensor_copy(out_tiles[q][:].indirect(slots), y_sb)
-
-        packed, sigs, h_packed, y_banks = {}, {}, {}, {}
-        planes = [(g, j) for g in range(PASSES) for j in range(PACK)]
-        final = 5 * E - 2
-        spare = keep.tile([P, PACK, WIDTH], F32, name="spare", align_bytes=64)
-        for s in range(final + 1):
-            e, n = divmod(s, 5)
-            if e == 0:
-                for plane in planes[PL[n] : PL[n + 1]]:
+            if first:
+                for plane in planes[:PLANES_AHEAD]:
                     gather_plane(*plane)
-            raw = load(w2[e] if n == 4 else rows_of(w1 if n < 2 else w3, e, n % 2))
-            if e == 0 and n in XQ:
-                quantize_tokens(XQ.index(n))
-            packed[s] = quantize_weights(raw, n < 4, ENG[e][n], "vector" in ENG[e][n])
-            for d in range(E):
-                if min(5 * d + SG[d], final) == s:
-                    sigmoid_step(d, raw)
-                if d < E - 1:
-                    if 5 * d + MU[d] == s:
-                        hidden_step(d, raw)
-                    for q in range(PACK):
-                        if min(5 * d + EV[d][q], final) == s:
-                            if q == 0:
-                                y_banks[d] = second_product(d, *packed[5 * d + 4], range(PACK))
-                            leave_step(d, q, y_banks[d], q, raw[:, 2, q * C : (q + 1) * C])
+                tag = "x_plane%d_%d" % planes[PLANES_AHEAD - 1]
+                codes = keep.tile([P, WIDTH], U32, name="first_codes", tag=tag, align_bytes=64)
+                scales = coded.tile([P, WIDTH], U8, name="scales", align_bytes=64)
+            else:
+                codes, scales = packed_tiles()
+            w1_packed = [pack_first_on_scalar(load(w1[e, 0:K_PASS, :]), codes, scales)]
 
-        halves = []
-        for u in range(2):
-            half = keep.tile([P, PACK, HALF], F32, name="w2_last%d" % u)
-            nc.sync.dma_start(
-                out=half[:], in_=w2[E - 1].rearrange("(p j) w -> p j w", j=PACK)[:, :, u * HALF : (u + 1) * HALF]
-            )
-            halves.append(half)
-        hidden_step(E - 1, None)
-        for u, half in enumerate(halves):
+            if first:
+                for plane in planes[PLANES_AHEAD : 2 * PLANES_AHEAD]:
+                    gather_plane(*plane)
+            raw = load(w1[e, K_PASS:K, :])
+            if first:
+                quantize_tokens(0, scalar_copy)
+                w1_packed.append(pack_first_on_scalar(raw, *packed_tiles()))
+            else:
+                w1_packed.append(pack_in_halves(raw, shared, reorder=True))
+                y_bank = second_product(h_packed, w2_packed, QUARTERS)
+                for q in range(QUARTERS - 1 if last else QUARTERS):
+                    scatter(e - 1, q, y_bank[:, q, :], raw[:, 2, q * C : (q + 1) * C])
+
+            if first:
+                for plane in planes[2 * PLANES_AHEAD :]:
+                    gather_plane(*plane)
+            raw = load(w3[e, 0:K_PASS, :])
+            if first:
+                quantize_tokens(1, vector_copy)
+            w3_packed = [pack_first_on_scalar(raw, *packed_tiles())]
+            if not last:
+                sig = raw[:, 0, :]
+                sigmoid_of(e, w1_packed, sig)
+
+            raw = load(w3[e, K_PASS:K, :])
+            if not last:
+                w3_packed.append(pack_in_halves(raw, (vector_copy, vector_copy), reorder=True))
+                h_packed = pack_hidden(e, w3_packed, sig, raw[:, 1, 0:HALF].bitcast(BF16))
+                w2_packed = pack_in_halves(load(w2[e]), shared, reorder=False)
+
+        w3_packed.append(pack_in_halves(raw, shared, reorder=True))
+        sig = raw[:, 0, :]
+        sigmoid_of(E - 1, w1_packed, sig)
+        scatter(E - 2, QUARTERS - 1, y_bank[:, QUARTERS - 1, :], raw[:, 2, 0:C])
+        w2_halves = [keep.tile([P, PACK, HALF], F32, name="w2_last%d" % u) for u in range(2)]
+        w2_rows = w2[E - 1].rearrange("(p j) w -> p j w", j=PACK)
+        for u, half in enumerate(w2_halves):
+            nc.sync.dma_start(out=half[:], in_=w2_rows[:, :, u * HALF : (u + 1) * HALF])
+        hidden = keep.tile([P, C * PACK], BF16, name="last_hidden", tag="handed_on", align_bytes=64)
+        h_packed = pack_hidden(E - 1, w3_packed, sig, hidden[:])
+
+        y_last = keep.tile([P, QUARTERS, C], F32, name="y_last")
+        for u, half in enumerate(w2_halves):
             grouped = stage.tile([P, PACK * HALF], BF16, name="grouped", align_bytes=64)
             if u == 0:
                 codes = coded.tile([P, HALF], U32, name="codes", align_bytes=64)
             else:
                 codes = keep.tile([P, HALF], U32, name="last_codes", tag="handed_on", align_bytes=64)
             scales = coded.tile([P, HALF], U8, name="scales", align_bytes=64)
-            copy_on(
-                ENG[E - 1][4][u],
-                grouped[:].rearrange("p (c i v w) -> p c v i w", i=4, v=2, w=2),
-                half[:].rearrange("p (v w) (c i) -> p c v i w", i=4, w=2),
-            )
+            round_and_group(scalar_copy, grouped[:], half[:])
             quantize(grouped[:], codes[:], scales[:])
-            bank = second_product(E - 1, codes, scales, range(2))
-            for place in range(2):
-                q = 2 * u + place
-                leave_step(E - 1, q, bank, place, spare[:, 2, q * C : (q + 1) * C])
+            y_bank = second_product(h_packed, (codes, scales), 2)
+            for b in range(2):
+                q = 2 * u + b
+                scatter(E - 1, q, y_bank[:, b, :], y_last[:, q, :])
                 nc.sync.dma_start(out=out[q * P : (q + 1) * P, :], in_=out_tiles[q][:])

from contextlib import ExitStack

import concourse.mybir as mybir
from concourse.masks import make_identity

K, T, E, C, H, N = 1024, 640, 4, 128, 512, 512
S = E * C

FLOPS = 2 * S * (2 * K * H + H * N)
BYTES = 4 * (K * T + 2 * E * K * H + E * H * N + S + N * T) + 2 * 128 * (S // 16)

F32 = mybir.dt.float32
BF16 = mybir.dt.bfloat16
U32 = mybir.dt.uint32
U16 = mybir.dt.uint16
U8 = mybir.dt.uint8
FP8X4 = mybir.dt.float8_e4m3fn_x4
MULT = mybir.AluOpType.mult
SIGMOID = mybir.ActivationFunctionType.Sigmoid

P = 128
PACK = 4
K_PASS = P * PACK
PASSES = K // K_PASS
WIDTH = 512
HALF = WIDTH // 2
QUARTERS = N // P
LIST_COLS = C // 16

PLANES_AHEAD = 3

RAW_BUFS, GROUPED_BUFS, PACKED_BUFS = 12, 5, 10


def tile_moe_pre_glu_sigmoid_kernel(tc, xT, w1, w3, w2, gate, offs, out):
    nc = tc.nc

    with ExitStack() as ctx:
        keep = ctx.enter_context(tc.tile_pool(name="keep", bufs=1))
        raws = ctx.enter_context(tc.tile_pool(name="raws", bufs=RAW_BUFS))
        stage = ctx.enter_context(tc.tile_pool(name="stage", bufs=GROUPED_BUFS))
        coded = ctx.enter_context(tc.tile_pool(name="coded", bufs=PACKED_BUFS))
        small = ctx.enter_context(tc.tile_pool(name="small", bufs=2))
        psum = ctx.enter_context(tc.psum_pool(name="psum", bufs=2))

        scalar_copy = nc.scalar.copy
        vector_copy = nc.vector.tensor_copy

        offsets = keep.tile([P, S // 16], U16, name="offsets")
        nc.sync.dma_start(offsets[:], offs)
        gate_sb = keep.tile([P, S], F32, name="gate_sb")

        warm = keep.tile([P, 1], F32, name="warm")
        nc.vector.memset(warm[:], 0.0)
        nc.scalar.activation(out=warm[:], in_=warm[:], func=SIGMOID)

        gate_cols = keep.tile([P, PACK], F32, name="gate_cols")
        nc.sync.dma_start(out=gate_cols[:], in_=gate[0:1, :].rearrange("o (p r) -> (o p) r", r=PACK))
        identity = keep.tile([P, P], F32, name="identity")
        make_identity(nc, identity[:])
        spread = psum.tile([P, PACK, P], F32, name="a_bank")
        for r in range(PACK):
            nc.tensor.transpose(spread[:, r, :], gate_cols[:, r : r + 1].to_broadcast([P, P]), identity[:])
        vector_copy(out=gate_sb[:].rearrange("q (p r) -> q p r", r=PACK), in_=spread[:].rearrange("q r p -> q p r"))

        out_tiles = [keep.tile([P, T], F32, name="out%d" % q) for q in range(QUARTERS)]
        for window in out_tiles:
            nc.gpsimd.memset(window[:], 0.0)

        def quantize(grouped, codes, scales):
            nc.vector.quantize_mx(out=codes.bitcast(FP8X4), scales=scales, in_=grouped)

        def round_and_group(copy, grouped, rows):
            copy(
                out=grouped.rearrange("p (c i v w) -> p c v i w", i=4, v=2, w=2),
                in_=rows.rearrange("p (v w) (c i) -> p c v i w", i=4, w=2),
            )

        def round_and_reorder(copy, grouped, raw, t0, t1):
            copy(
                out=grouped[:, t0 * PACK * P : t1 * PACK * P].rearrange("p (t m v w) -> p m v t w", m=P, v=2, w=2),
                in_=raw.rearrange("p (v w) (m t) -> p m v t w", t=PACK, w=2)[:, :, :, t0:t1, :],
            )

        x_rows = xT.rearrange("(g p j) t -> g j p t", p=P, j=PACK)
        gathered = [keep.tile([P, PACK, S], F32, name="gathered%d" % g) for g in range(PASSES)]
        x_codes = [keep.tile([P, S], U32, name="x_codes%d" % g, align_bytes=64) for g in range(PASSES)]
        x_scales = [keep.tile([P, S], U8, name="x_scales%d" % g, align_bytes=64) for g in range(PASSES)]
        planes = [(g, j) for g in range(PASSES) for j in range(PACK)]

        def gather_plane(g, j):
            plane = keep.tile([P, T], F32, name="x_plane%d_%d" % (g, j), align_bytes=64)
            nc.sync.dma_start(out=plane[:], in_=x_rows[g, j])
            nc.vector.tensor_tensor(gathered[g][:, j, :], plane[:].indirect(offsets[:]), gate_sb[:], MULT)

        def quantize_tokens(g, copy):
            grouped = stage.tile([P, PACK * S], BF16, name="grouped", align_bytes=64)
            round_and_group(copy, grouped[:], gathered[g][:])
            quantize(grouped[:], x_codes[g][:], x_scales[g][:])

        def load(rows):
            raw = raws.tile([P, PACK, WIDTH], F32, name="raw", align_bytes=64)
            nc.sync.dma_start(out=raw[:], in_=rows.rearrange("(p j) w -> p j w", j=PACK))
            return raw

        def packed_tiles():
            codes = coded.tile([P, WIDTH], U32, name="codes", align_bytes=64)
            scales = coded.tile([P, WIDTH], U8, name="scales", align_bytes=64)
            return codes, scales

        def pack_first_on_scalar(raw, codes, scales):
            grouped = stage.tile([P, PACK * WIDTH], BF16, name="grouped", align_bytes=64)
            round_and_reorder(scalar_copy, grouped[:], raw[:], 0, PACK)
            quantize(grouped[:], codes[:], scales[:])
            return codes, scales

        def pack_in_halves(raw, copies, reorder):
            grouped = stage.tile([P, PACK * WIDTH], BF16, name="grouped", align_bytes=64)
            codes, scales = packed_tiles()
            halves = [slice(u * HALF, (u + 1) * HALF) for u in range(2)]
            grouped_halves = [grouped[:, u * PACK * HALF : (u + 1) * PACK * HALF] for u in range(2)]
            for u, copy in enumerate(copies):
                if reorder:
                    round_and_reorder(copy, grouped[:], raw[:], 2 * u, 2 * u + 2)
                else:
                    round_and_group(copy, grouped_halves[u], raw[:, :, halves[u]])
            for u in range(2):
                quantize(grouped_halves[u], codes[:, halves[u]], scales[:, halves[u]])
            return codes, scales

        def first_product(e, weights, name):
            bank = psum.tile([P, PACK, C], F32, name=name)
            slots = slice(e * C, (e + 1) * C)
            for t in range(PACK):
                for g, (codes, scales) in enumerate(weights):
                    nc.tensor.matmul_mx(
                        out=bank[:, t, :],
                        lhsT=codes[:, t * P : (t + 1) * P].bitcast(FP8X4),
                        lhsT_scale=scales[:, t * P : (t + 1) * P],
                        rhs=x_codes[g][:, slots].bitcast(FP8X4),
                        rhs_scale=x_scales[g][:, slots],
                        start=(g == 0),
                        stop=(g == PASSES - 1),
                    )
            return bank

        def sigmoid_of(e, weights, room):
            a_bank = first_product(e, weights, "a_bank")
            nc.scalar.activation(
                out=room.rearrange("p (c t) -> p c t", t=PACK),
                in_=a_bank[:].rearrange("p t c -> p c t"),
                func=SIGMOID,
            )

        def pack_hidden(e, weights, sig, hidden):
            b_bank = first_product(e, weights, "b_bank")
            nc.vector.tensor_tensor(
                hidden.rearrange("p (c t) -> p c t", t=PACK),
                b_bank[:].rearrange("p t c -> p c t"),
                sig.rearrange("p (c t) -> p c t", t=PACK),
                MULT,
            )
            h_codes = small.tile([P, C], U32, name="h_codes", align_bytes=64)
            h_scales = small.tile([P, C], U8, name="h_scales", align_bytes=64)
            quantize(hidden, h_codes[:], h_scales[:])
            return h_codes, h_scales

        def second_product(h_packed, weights, blocks):
            codes, scales = weights
            bank = psum.tile([P, blocks, C], F32, name="y_bank")
            for b in range(blocks):
                nc.tensor.matmul_mx(
                    out=bank[:, b, :],
                    lhsT=codes[:, b * P : (b + 1) * P].bitcast(FP8X4),
                    lhsT_scale=scales[:, b * P : (b + 1) * P],
                    rhs=h_packed[0][:].bitcast(FP8X4),
                    rhs_scale=h_packed[1][:],
                    start=True,
                    stop=True,
                )
            return bank

        def scatter(e, q, y_psum, room):
            scalar_copy(out=room, in_=y_psum)
            vector_copy(out_tiles[q][:].indirect(offsets[:, e * LIST_COLS : (e + 1) * LIST_COLS]), room)

        shared = (vector_copy, scalar_copy)
        h_packed = w2_packed = None
        for e in range(E):
            first = e == 0
            last = e == E - 1

            if first:
                for plane in planes[:PLANES_AHEAD]:
                    gather_plane(*plane)
                tag = "x_plane%d_%d" % planes[PLANES_AHEAD - 1]
                codes = keep.tile([P, WIDTH], U32, name="first_codes", tag=tag, align_bytes=64)
                scales = coded.tile([P, WIDTH], U8, name="scales", align_bytes=64)
            else:
                codes, scales = packed_tiles()
            w1_packed = [pack_first_on_scalar(load(w1[e, 0:K_PASS, :]), codes, scales)]

            if first:
                for plane in planes[PLANES_AHEAD : 2 * PLANES_AHEAD]:
                    gather_plane(*plane)
            raw = load(w1[e, K_PASS:K, :])
            if first:
                quantize_tokens(0, scalar_copy)
                w1_packed.append(pack_first_on_scalar(raw, *packed_tiles()))
            else:
                w1_packed.append(pack_in_halves(raw, shared, reorder=True))
                y_bank = second_product(h_packed, w2_packed, QUARTERS)
                for q in range(QUARTERS - 1 if last else QUARTERS):
                    scatter(e - 1, q, y_bank[:, q, :], raw[:, 2, q * C : (q + 1) * C])

            if first:
                for plane in planes[2 * PLANES_AHEAD :]:
                    gather_plane(*plane)
            raw = load(w3[e, 0:K_PASS, :])
            if first:
                quantize_tokens(1, vector_copy)
            w3_packed = [pack_first_on_scalar(raw, *packed_tiles())]
            if not last:
                sig = raw[:, 0, :]
                sigmoid_of(e, w1_packed, sig)

            raw = load(w3[e, K_PASS:K, :])
            if not last:
                w3_packed.append(pack_in_halves(raw, (vector_copy, vector_copy), reorder=True))
                h_packed = pack_hidden(e, w3_packed, sig, raw[:, 1, 0:HALF].bitcast(BF16))
                w2_packed = pack_in_halves(load(w2[e]), shared, reorder=False)

        w3_packed.append(pack_in_halves(raw, shared, reorder=True))
        sig = raw[:, 0, :]
        sigmoid_of(E - 1, w1_packed, sig)
        scatter(E - 2, QUARTERS - 1, y_bank[:, QUARTERS - 1, :], raw[:, 2, 0:C])
        w2_halves = [keep.tile([P, PACK, HALF], F32, name="w2_last%d" % u) for u in range(2)]
        w2_rows = w2[E - 1].rearrange("(p j) w -> p j w", j=PACK)
        for u, half in enumerate(w2_halves):
            nc.sync.dma_start(out=half[:], in_=w2_rows[:, :, u * HALF : (u + 1) * HALF])
        hidden = keep.tile([P, C * PACK], BF16, name="last_hidden", tag="handed_on", align_bytes=64)
        h_packed = pack_hidden(E - 1, w3_packed, sig, hidden[:])

        y_last = keep.tile([P, QUARTERS, C], F32, name="y_last")
        for u, half in enumerate(w2_halves):
            grouped = stage.tile([P, PACK * HALF], BF16, name="grouped", align_bytes=64)
            if u == 0:
                codes = coded.tile([P, HALF], U32, name="codes", align_bytes=64)
            else:
                codes = keep.tile([P, HALF], U32, name="last_codes", tag="handed_on", align_bytes=64)
            scales = coded.tile([P, HALF], U8, name="scales", align_bytes=64)
            round_and_group(scalar_copy, grouped[:], half[:])
            quantize(grouped[:], codes[:], scales[:])
            y_bank = second_product(h_packed, (codes, scales), 2)
            for b in range(2):
                q = 2 * u + b
                scatter(E - 1, q, y_bank[:, b, :], y_last[:, q, :])
                nc.sync.dma_start(out=out[q * P : (q + 1) * P, :], in_=out_tiles[q][:])
